import numpy as np
import ml_dtypes


def mxq(x, axis, fmt="e4m3"):
    dtype, down = {"e4m3": (ml_dtypes.float8_e4m3fn, 7), "e5m2": (ml_dtypes.float8_e5m2, 14)}[fmt]
    v = np.moveaxis(np.asarray(x, np.float32).astype(ml_dtypes.bfloat16).astype(np.float64), axis, -1)
    blocks = v.reshape(v.shape[:-1] + (-1, 32))
    amax = np.abs(blocks).max(-1, keepdims=True)
    byte = np.maximum(np.where(amax > 0, np.frexp(amax)[1] - 1 + 127, 0) - down, 1)
    scale = np.exp2(byte - 127.0)
    codes = (blocks / scale).astype(np.float32).astype(dtype).astype(np.float64)
    return np.moveaxis((codes * scale).reshape(v.shape), -1, axis)


WIDE = False


def mx_kscale(k):
    if not WIDE:
        return np.ones(k)
    levels = np.array([10, -10, 5, -5, 0])
    if k % 512:
        return np.exp2(np.random.permutation(np.resize(levels, k // 32))).repeat(32)
    a = np.empty((k // 512, 16))
    for p in range(k // 512):
        a[p, :8] = np.random.permutation(np.resize(levels, 8))
        for g in range(8):
            far = levels[np.abs(levels - a[p, g]) >= 10]
            a[p, g + 8] = far[np.random.randint(len(far))]
    return np.exp2(a.ravel()).repeat(32)


def f64(x):
    return np.asarray(x).astype(np.float64)


def striped(idx):
    return np.tile(idx.reshape(-1, 16).T, (8, 1)).astype(np.uint16)


def unstriped(offs):
    return offs[:16].T.reshape(-1).astype(np.int64)


def striped8(idx):
    return np.concatenate([x.reshape(-1, 16).T for x in idx]).astype(np.uint16)


def runs(offs, k):
    lists = np.stack([offs[16 * r : 16 * r + 16].T.reshape(-1) for r in range(8)]).astype(np.int64)
    return lists[np.arange(k) % 512 // 64]


def pack_weight(w):
    k, n = w.shape
    w = f64(np.asarray(w, np.float32).astype(ml_dtypes.bfloat16)).reshape(k // 32, 32, n)
    amax = np.abs(w).max(1)
    byte = np.clip(np.where(amax > 0, np.frexp(amax)[1] - 1 + 127 - 7, 1), 1, 254)
    scaled = (w * np.exp2(127.0 - byte)[:, None, :]).reshape(k, n).astype(np.float32)
    words = np.ascontiguousarray(scaled.reshape(k // 512, 128, 4, n).transpose(0, 1, 3, 2)).astype(ml_dtypes.float8_e4m3fn).view(np.uint8)
    return words, np.ascontiguousarray(byte.astype(np.uint8).reshape(k // 512, 16, n))


def unpack_weight(words, scales):
    g, p, n, _ = words.shape
    vals = np.ascontiguousarray(words).view(ml_dtypes.float8_e4m3fn).astype(np.float64) * np.repeat(np.exp2(scales.astype(np.float64) - 127.0), 8, axis=1)[..., None]
    return vals.transpose(0, 1, 3, 2).reshape(g * 512, n)


E2M1 = np.array([0.0, 0.5, 1.0, 1.5, 2.0, 3.0, 4.0, 6.0, -0.0, -0.5, -1.0, -1.5, -2.0, -3.0, -4.0, -6.0])


def pack_fp4(w):
    k, n = w.shape
    w = f64(np.asarray(w, np.float32).astype(ml_dtypes.bfloat16)).reshape(k // 32, 32, n)
    amax = np.abs(w).max(1)
    mant, ex = np.frexp(amax / 6.0)
    byte = np.clip(np.where(amax > 0, np.where(mant > 0.5, ex, ex - 1) + 127, 1), 1, 254)
    scaled = (w * np.exp2(127.0 - byte)[:, None, :]).reshape(k, n).astype(np.float32)
    c = np.ascontiguousarray(scaled.reshape(k // 512, 128, 4, n).transpose(0, 1, 3, 2)).astype(ml_dtypes.float4_e2m1fn).view(np.uint8) & 0xF
    words = (c[..., 0::2] | (c[..., 1::2] << 4)).reshape(k // 512, 128, 2 * n)
    return np.ascontiguousarray(words), np.ascontiguousarray(byte.astype(np.uint8).reshape(k // 512, 16, n))


def unpack_fp4(words, scales):
    g, _, n = scales.shape
    words = np.ascontiguousarray(words).reshape(g, 128, n, 2)
    nib = np.empty((g, 128, n, 4), np.uint8)
    nib[..., 0::2] = words & 0xF
    nib[..., 1::2] = words >> 4
    vals = E2M1[nib] * np.repeat(np.exp2(scales.astype(np.float64) - 127.0), 8, axis=1)[..., None]
    return vals.transpose(0, 1, 3, 2).reshape(g * 512, n)


def planes(y):
    n, m = y.shape
    v = y.astype(np.float32).astype(ml_dtypes.bfloat16).astype(np.float64).reshape(n // 32, 32, m)
    top = np.abs(v).max(1)
    byte = np.clip(np.where(top > 0, np.frexp(top)[1] - 1 + 127 - 7, 1), 1, 254)
    codes = (v * np.exp2(127.0 - byte)[:, None, :]).reshape(n, m).astype(np.float32).astype(ml_dtypes.float8_e4m3fn).view(np.uint8)
    words = codes.reshape(n // 512, 128, 4, m).transpose(0, 1, 3, 2)
    return np.ascontiguousarray(words), np.ascontiguousarray(byte.astype(np.uint8).reshape(n // 512, 16, m))


K, T, S, V, N, H = 512, 2048, 512, 256, 512, 512


def setup_inputs():
    n = np.random.standard_normal
    s = mx_kscale(K)[:, None]
    u = mx_kscale(H)
    packed_xT = pack_weight(n((K, T)) * s)
    packed_w3 = pack_fp4(n((H, N)) / np.sqrt(H) / u[:, None])
    perm = np.stack([np.random.permutation(S) for _ in range(8)])
    perm2 = np.stack([np.random.permutation(S) for _ in range(8)])
    return {
        "x_words": packed_xT[0],
        "x_scales": packed_xT[1],
        "w1": (n((K, H)) / np.sqrt(K) / s * u).astype(np.float32),
        "w2": (n((H, H)) / np.sqrt(H) / u[:, None] * u).astype(np.float32),
        "w3_words": packed_w3[0],
        "w3_scales": packed_w3[1],
        "res": n((N, S)).astype(np.float32),
        "offs": striped(np.random.permutation(T)[:S]),
        "la": striped8(perm[:, :V]),
        "lb": striped8(perm[:, V:]),
        "ma": striped8(perm2[:, :V]),
        "mb": striped8(perm2[:, V:]),
    }


def reference(x_words, x_scales, w1, w2, w3_words, w3_scales, res, offs, la, lb, ma, mb):
    xq = unpack_weight(x_words, x_scales)[:, unstriped(offs)]
    y = mxq(f64(w1), 0, "e4m3").T @ xq
    nb = 0.5 * (y[np.arange(H)[:, None], runs(la, H)] + y[np.arange(H)[:, None], runs(lb, H)])
    na = y[np.arange(H)[:, None], runs(lb, H)] - (y[np.arange(H)[:, None], runs(la, H)])
    p0 = np.zeros((H, S))
    p0[np.arange(H)[:, None], runs(la, H)] = na
    z = p0.copy()
    z[np.arange(H)[:, None], runs(lb, H)] = nb
    h = mxq(f64(w2), 0, "e4m3").T @ mxq(z, 0, "e4m3")
    rb = np.minimum(h[np.arange(H)[:, None], runs(ma, H)], h[np.arange(H)[:, None], runs(mb, H)])
    ra = np.maximum(h[np.arange(H)[:, None], runs(ma, H)], h[np.arange(H)[:, None], runs(mb, H)])
    q0 = np.zeros((H, S))
    q0[np.arange(H)[:, None], runs(ma, H)] = ra
    z2 = q0.copy()
    z2[np.arange(H)[:, None], runs(mb, H)] = rb
    out_0 = f64(res) + (unpack_fp4(w3_words, w3_scales).T @ mxq(z2, 0, "e4m3"))
    return (out_0,) + planes(out_0)

@@ -1,0 +1,263 @@
+from contextlib import ExitStack
+
+import concourse.mybir as mybir
+
+F32 = mybir.dt.float32
+BF16 = mybir.dt.bfloat16
+I32 = mybir.dt.int32
+U32 = mybir.dt.uint32
+U16 = mybir.dt.uint16
+U8 = mybir.dt.uint8
+FP8X4 = mybir.dt.float8_e4m3fn_x4
+FP4X4 = mybir.dt.float4_e2m1fn_x4
+ALU = mybir.AluOpType
+COPY = mybir.ActivationFunctionType.Copy
+
+P = 128
+PACK = 4
+T = 2048
+S = 512
+V = 256
+HALF = 256
+CH = 128
+FLOPS = 3 * 2 * 512 * 512 * 512
+
+
+def tile_picked_lifted_none_po_kernel(
+    tc, x_words, x_scales, w1, w2, w3_words, w3_scales, res, offs, la, lb, ma, mb, out_0, out_1, out_2
+):
+    nc = tc.nc
+    with ExitStack() as ctx:
+        lists = ctx.enter_context(tc.tile_pool(name="lists", bufs=1))
+        keep = ctx.enter_context(tc.tile_pool(name="keep", bufs=1))
+        psum = ctx.enter_context(tc.psum_pool(name="psum", bufs=1))
+
+        def sb(name, shape, dtype):
+            return keep.tile(shape, dtype, name=name, align_bytes=64)
+
+        def bank(n, shape):
+            return psum.tile(shape, F32, name="bank%d" % n)
+
+        offs_sb = lists.tile([P, S // 16], U16, name="offs_sb")
+        la_sb = lists.tile([P, V // 16], U16, name="la_sb")
+        lb_sb = lists.tile([P, V // 16], U16, name="lb_sb")
+        ma_sb = lists.tile([P, V // 16], U16, name="ma_sb")
+        mb_sb = lists.tile([P, V // 16], U16, name="mb_sb")
+
+        x_w = sb("x_w", [P, T], U32)
+        x_s = sb("x_s", [P, T], U8)
+        w3_w = sb("w3_w", [P, 2 * S], U8)
+        w3_s = sb("w3_s", [P, S], U8)
+
+        def load_halves(src):
+            tiles = []
+            for u in range(2):
+                raw = sb("raw%d" % u, [P, PACK, HALF], F32)
+                nc.sync.dma_start(raw[:], src.rearrange("(p j) c -> p j c", j=PACK)[:, :, u * HALF : (u + 1) * HALF])
+                tiles.append(raw)
+            return tiles
+
+        nc.gpsimd.memset(x_s[:].bitcast(I32), 0)
+        nc.vector.memset(w3_s[:].bitcast(I32), 0)
+        for q in range(4):
+            nc.scalar.dma_start(x_s[32 * q : 32 * q + 4, :].bitcast(I32), x_scales[0, 4 * q : 4 * q + 4, :].bitcast(I32))
+        nc.sync.dma_start(offs_sb[:], offs)
+        nc.sync.dma_start(la_sb[:], la)
+        nc.sync.dma_start(lb_sb[:], lb)
+        nc.sync.dma_start(ma_sb[:], ma)
+        nc.sync.dma_start(x_w[:].bitcast(I32), x_words[0].rearrange("p n t -> p (n t)").bitcast(I32))
+        w1_raw = load_halves(w1)
+        nc.sync.dma_start(mb_sb[:], mb)
+        nc.gpsimd.dma_start(w3_w[:].bitcast(I32), w3_words[0].bitcast(I32))
+        for q in range(4):
+            nc.gpsimd.dma_start(w3_s[32 * q : 32 * q + 4, :].bitcast(I32), w3_scales[0, 4 * q : 4 * q + 4, :].bitcast(I32))
+
+        g_w = sb("g_w", [P, S], U32)
+        g_s = sb("g_s", [P, S], U8)
+        nc.vector.tensor_copy(g_w[:], x_w[:].indirect(offs_sb[:]))
+        nc.vector.tensor_copy(g_s[:], x_s[:].indirect(offs_sb[:]))
+
+        def deal(copy, grouped, raw, u, m0, m1):
+            dst = grouped[:].rearrange("p (t m j) -> p m t j", t=PACK, j=PACK)
+            src = raw[u][:].rearrange("p j (m t) -> p m t j", t=PACK)
+            copy(dst[:, 64 * u + m0 : 64 * u + m1], src[:, m0:m1])
+
+        def quant(codes, scales, grouped, c0, c1):
+            nc.vector.quantize_mx(out=codes[:, c0:c1].bitcast(FP8X4), scales=scales[:, c0:c1], in_=grouped[:, PACK * c0 : PACK * c1])
+
+        def product(out, w_codes, w_scales, t, codes, scales, c0, c1):
+            nc.tensor.matmul_mx(
+                out=out,
+                lhsT=w_codes[:, P * t : P * (t + 1)].bitcast(FP8X4),
+                lhsT_scale=w_scales[:, P * t : P * (t + 1)],
+                rhs=codes[:, c0:c1].bitcast(FP8X4),
+                rhs_scale=scales[:, c0:c1],
+                start=True,
+                stop=True,
+            )
+
+        w1_g = sb("w1_g", [P, PACK * S], BF16)
+        w1_c = sb("w1_c", [P, S], U32)
+        w1_s = sb("w1_s", [P, S], U8)
+        deal(nc.scalar.copy, w1_g, w1_raw, 0, 0, 64)
+        deal(nc.vector.tensor_copy, w1_g, w1_raw, 1, 0, 64)
+        for t in range(PACK):
+            quant(w1_c, w1_s, w1_g, P * t, P * (t + 1))
+
+        w2_raw = load_halves(w2)
+        w3_dw = sb("w3_dw", [P, 2 * S], U8)
+
+        w2_g = sb("w2_g", [P, PACK * S], BF16)
+        w2_c = sb("w2_c", [P, S], U32)
+        w2_s = sb("w2_s", [P, S], U8)
+
+        def layer(name, w_codes, w_scales, codes, scales, scale):
+            rows = []
+            for t in range(PACK):
+                row = sb("%s%d" % (name, t), [P, S], F32)
+                rows.append(row)
+                if t == 0:
+                    for u in range(2):
+                        acc = bank(u, [P, HALF])
+                        product(acc[:], w_codes, w_scales, t, codes, scales, u * HALF, (u + 1) * HALF)
+                        if u == 0:
+                            nc.scalar.activation(row[:, :HALF], acc[:], COPY, scale=scale)
+                        else:
+                            nc.vector.tensor_scalar(row[:, HALF:], acc[:], scale, None, ALU.mult)
+                else:
+                    acc = bank(t + 1, [P, S])
+                    product(acc[:], w_codes, w_scales, t, codes, scales, 0, S)
+                    rows.append(acc)
+            return rows
+
+        def fetch(name, t, row, acc, scale, first, second):
+            a = sb("%s_a%d" % (name, t), [P, V], F32)
+            b = sb("%s_b%d" % (name, t), [P, V], F32)
+            if t > 0:
+                nc.scalar.activation(row[:], acc[:], COPY, scale=scale)
+            nc.scalar.activation(a[:], row[:].indirect(first[:]), COPY)
+            if t == 0:
+                nc.vector.tensor_copy(b[:], row[:].indirect(second[:]))
+            else:
+                nc.scalar.activation(b[:], row[:].indirect(second[:]), COPY)
+            return a, b
+
+        def plane(copy, grouped, z, t, c0, c1):
+            copy(grouped[:].rearrange("p (c j) -> p c j", j=PACK)[:, c0:c1, t], z[:, c0:c1])
+
+        def early_plane(grouped, z, t):
+            if t < 2:
+                plane(nc.scalar.copy, grouped, z, t, 0, S)
+            else:
+                plane(nc.vector.tensor_copy, grouped, z, t, 0, HALF)
+                plane(nc.scalar.copy, grouped, z, t, HALF, S)
+
+        def last_plane(grouped, z, codes, scales):
+            for c in range(4):
+                plane(nc.vector.tensor_copy if c < 2 else nc.scalar.copy, grouped, z, 3, CH * c, CH * (c + 1))
+            for c in range(4):
+                quant(codes, scales, grouped, CH * c, CH * (c + 1))
+
+        r = layer("y", w1_c, w1_s, g_w, g_s, 0.5)
+        rows = [r[0], r[1], r[3], r[5]]
+        accs = [None, r[2], r[4], r[6]]
+        z = [sb("z%d" % t, [P, S], F32) for t in range(PACK)]
+        z_g = sb("z_g", [P, PACK * S], BF16)
+        z_c = sb("z_c", [P, S], U32)
+        z_s = sb("z_s", [P, S], U8)
+        nc.scalar.copy(
+            w3_dw[:].bitcast(U16).rearrange("p (t m) -> p m t", t=PACK), w3_w[:].bitcast(U16).rearrange("p (m t) -> p m t", t=PACK)
+        )
+        ab = {}
+
+        def mean(t):
+            a, b = fetch("y", t, rows[t], accs[t], 0.5, la_sb, lb_sb)
+            ab[t] = (a, b)
+            nc.vector.tensor_tensor(z[t][:].indirect(lb_sb[:]), a[:], b[:], ALU.add)
+
+        def diff(t):
+            a, b = ab[t]
+            na = sb("na%d" % t, [P, V], F32)
+            pb = sb("pb%d" % t, [P, V], F32)
+            nc.scalar.activation(na[:], a[:], COPY, scale=-2.0)
+            nc.scalar.activation(pb[:], b[:], COPY, scale=2.0)
+            nc.vector.tensor_tensor(z[t][:].indirect(la_sb[:]), pb[:], na[:], ALU.add)
+
+        mean(0)
+        mean(1)
+        diff(0)
+        mean(2)
+        diff(1)
+        mean(3)
+        early_plane(z_g, z[0], 0)
+        diff(2)
+        deal(nc.scalar.copy, w2_g, w2_raw, 0, 0, 32)
+        early_plane(z_g, z[1], 1)
+        diff(3)
+        deal(nc.scalar.copy, w2_g, w2_raw, 0, 32, 64)
+        deal(nc.scalar.copy, w2_g, w2_raw, 1, 0, 32)
+        deal(nc.vector.tensor_copy, w2_g, w2_raw, 1, 32, 64)
+        early_plane(z_g, z[2], 2)
+        quant(w2_c, w2_s, w2_g, 0, P)
+        res_sb = load_halves(res)
+        last_plane(z_g, z[3], z_c, z_s)
+        for t in range(1, PACK):
+            quant(w2_c, w2_s, w2_g, P * t, P * (t + 1))
+        w3_ds = sb("z_g", [P, S], U8)
+        nc.vector.tensor_copy(
+            w3_ds[:].rearrange("p (t m) -> p t m", t=PACK), w3_s[:].rearrange("p (m t) -> p t m", t=PACK)
+        )
+
+        r = layer("h", w2_c, w2_s, z_c, z_s, 1.0)
+        rows = [r[0], r[1], r[3], r[5]]
+        accs = [None, r[2], r[4], r[6]]
+        z2 = [sb("zz%d" % t, [P, S], F32) for t in range(PACK)]
+        z2_g = sb("z2_g", [P, PACK * S], BF16)
+        z2_c = sb("z2_c", [P, S], U32)
+        z2_s = sb("z2_s", [P, S], U8)
+        low = {}
+        for t in range(PACK + 1):
+            if t < PACK:
+                a, b = fetch("h", t, rows[t], accs[t], 1.0, ma_sb, mb_sb)
+                hi = sb("hi%d" % t, [P, V], F32)
+                lo = sb("lo%d" % t, [P, V], F32)
+                low[t] = lo
+                nc.vector.tensor_tensor(hi[:], a[:], b[:], ALU.max)
+                nc.vector.tensor_tensor(lo[:], a[:], b[:], ALU.min)
+                nc.vector.tensor_copy(z2[t][:].indirect(ma_sb[:]), hi[:])
+            if t > 0:
+                nc.vector.tensor_copy(z2[t - 1][:].indirect(mb_sb[:]), low[t - 1][:])
+            if t > 1:
+                early_plane(z2_g, z2[t - 2], t - 2)
+        last_plane(z2_g, z2[3], z2_c, z2_s)
+
+        o_g = sb("o_g", [P, PACK * S], BF16)
+        o_c = sb("o_c", [P, S], U32)
+        o_s = sb("o_s", [P, S], U8)
+        out_rows = out_0.rearrange("(p t) j -> p t j", t=PACK)
+        out_words = out_1[0].rearrange("p n t -> p (n t)").bitcast(I32)
+        for c in range(4):
+            cols = slice(CH * c, CH * (c + 1))
+            acc = bank(c + 4 if c > 0 else 0, [P, PACK, CH])
+            for t in range(PACK):
+                nc.tensor.matmul_mx(
+                    out=acc[:, t, :],
+                    lhsT=w3_dw[:, 2 * P * t : 2 * P * (t + 1)].bitcast(FP4X4),
+                    lhsT_scale=w3_ds[:, P * t : P * (t + 1)],
+                    rhs=z2_c[:, cols].bitcast(FP8X4),
+                    rhs_scale=z2_s[:, cols],
+                    start=True,
+                    stop=True,
+                )
+            o = sb("o%d" % c, [P, PACK, CH], F32)
+            nc.vector.tensor_tensor(o[:], acc[:], res_sb[c // 2][:, :, CH * (c % 2) : CH * (c % 2 + 1)], ALU.add)
+            nc.sync.dma_start(out_rows[:, :, cols], o[:])
+            nc.scalar.copy(
+                o_g[:, PACK * CH * c : PACK * CH * (c + 1)].rearrange("p (c i t) -> p c t i", i=4, t=PACK),
+                o[:].rearrange("p t (c i) -> p c t i", i=4),
+            )
+            quant(o_c, o_s, o_g, CH * c, CH * (c + 1))
+            nc.sync.dma_start(out_words[:, cols], o_c[:, cols].bitcast(I32))
+        for q in range(4):
+            eng = nc.sync if q % 2 == 0 else nc.scalar
+            eng.dma_start(out_2[0, 4 * q : 4 * q + 4, :].bitcast(I32), o_s[32 * q : 32 * q + 4, :].bitcast(I32))

@@ -12,6 +12,7 @@ FP8X4 = mybir.dt.float8_e4m3fn_x4
 FP4X4 = mybir.dt.float4_e2m1fn_x4
 ALU = mybir.AluOpType
 COPY = mybir.ActivationFunctionType.Copy
+RELU = mybir.ActivationFunctionType.Relu
 
 P = 128
 PACK = 4
@@ -46,7 +47,6 @@ def tile_picked_lifted_none_po_kernel(
 
         x_w = sb("x_w", [P, T], U32)
         x_s = sb("x_s", [P, T], U8)
-        w3_w = sb("w3_w", [P, 2 * S], U8)
         w3_s = sb("w3_s", [P, S], U8)
 
         def load_halves(src):
@@ -59,28 +59,33 @@ def tile_picked_lifted_none_po_kernel(
 
         nc.gpsimd.memset(x_s[:].bitcast(I32), 0)
         nc.vector.memset(w3_s[:].bitcast(I32), 0)
+        nc.gpsimd.dma_start(w3_s[0:16, :].bitcast(I32), w3_scales[0].bitcast(I32))
+        w3_ds = sb("w3_ds", [P, S], U8)
+        nc.gpsimd.memset(w3_ds[:].bitcast(I32), 0)
         for q in range(4):
             nc.scalar.dma_start(x_s[32 * q : 32 * q + 4, :].bitcast(I32), x_scales[0, 4 * q : 4 * q + 4, :].bitcast(I32))
         nc.sync.dma_start(offs_sb[:], offs)
         nc.sync.dma_start(la_sb[:], la)
         nc.sync.dma_start(lb_sb[:], lb)
         nc.sync.dma_start(ma_sb[:], ma)
-        nc.sync.dma_start(x_w[:].bitcast(I32), x_words[0].rearrange("p n t -> p (n t)").bitcast(I32))
         w1_raw = load_halves(w1)
+        nc.sync.dma_start(x_w[:].bitcast(I32), x_words[0].rearrange("p n t -> p (n t)").bitcast(I32))
         nc.sync.dma_start(mb_sb[:], mb)
-        nc.gpsimd.dma_start(w3_w[:].bitcast(I32), w3_words[0].bitcast(I32))
+        w3_rows = sb("w3_rows", [P, S], U8)
+        nc.vector.tensor_copy(
+            w3_rows[:].rearrange("p (t m) -> p t m", t=PACK), w3_s[:].rearrange("p (m t) -> p t m", t=PACK)
+        )
         for q in range(4):
-            nc.gpsimd.dma_start(w3_s[32 * q : 32 * q + 4, :].bitcast(I32), w3_scales[0, 4 * q : 4 * q + 4, :].bitcast(I32))
+            nc.sync.dma_start(w3_ds[32 * q : 32 * q + 4, :].bitcast(I32), w3_rows[4 * q : 4 * q + 4, :].bitcast(I32))
 
         g_w = sb("g_w", [P, S], U32)
         g_s = sb("g_s", [P, S], U8)
-        nc.vector.tensor_copy(g_w[:], x_w[:].indirect(offs_sb[:]))
         nc.vector.tensor_copy(g_s[:], x_s[:].indirect(offs_sb[:]))
 
-        def deal(copy, grouped, raw, u, m0, m1):
+        def deal(copy, grouped, raw, u, m0, m1, t0=0, t1=PACK):
             dst = grouped[:].rearrange("p (t m j) -> p m t j", t=PACK, j=PACK)
             src = raw[u][:].rearrange("p j (m t) -> p m t j", t=PACK)
-            copy(dst[:, 64 * u + m0 : 64 * u + m1], src[:, m0:m1])
+            copy(dst[:, 64 * u + m0 : 64 * u + m1, t0:t1], src[:, m0:m1, t0:t1])
 
         def quant(codes, scales, grouped, c0, c1):
             nc.vector.quantize_mx(out=codes[:, c0:c1].bitcast(FP8X4), scales=scales[:, c0:c1], in_=grouped[:, PACK * c0 : PACK * c1])
@@ -101,31 +106,31 @@ def tile_picked_lifted_none_po_kernel(
         w1_s = sb("w1_s", [P, S], U8)
         deal(nc.scalar.copy, w1_g, w1_raw, 0, 0, 64)
         deal(nc.vector.tensor_copy, w1_g, w1_raw, 1, 0, 64)
-        for t in range(PACK):
-            quant(w1_c, w1_s, w1_g, P * t, P * (t + 1))
+        quant(w1_c, w1_s, w1_g, 0, S)
+        for c in range(4):
+            nc.vector.tensor_copy(g_w[:, CH * c : CH * (c + 1)], x_w[:].indirect(offs_sb[:, 8 * c : 8 * (c + 1)]))
 
         w2_raw = load_halves(w2)
-        w3_dw = sb("w3_dw", [P, 2 * S], U8)
 
-        w2_g = sb("w2_g", [P, PACK * S], BF16)
         w2_c = sb("w2_c", [P, S], U32)
         w2_s = sb("w2_s", [P, S], U8)
 
-        def layer(name, w_codes, w_scales, codes, scales, scale):
+        def layer(name, w_codes, w_scales, codes, scales, scale, parts):
             rows = []
             for t in range(PACK):
                 row = sb("%s%d" % (name, t), [P, S], F32)
                 rows.append(row)
                 if t == 0:
-                    for u in range(2):
-                        acc = bank(u, [P, HALF])
-                        product(acc[:], w_codes, w_scales, t, codes, scales, u * HALF, (u + 1) * HALF)
-                        if u == 0:
-                            nc.scalar.activation(row[:, :HALF], acc[:], COPY, scale=scale)
+                    width = S // parts
+                    for u in range(parts):
+                        acc = bank(u, [P, width])
+                        product(acc[:], w_codes, w_scales, t, codes, scales, u * width, (u + 1) * width)
+                        if u < parts - 1:
+                            nc.scalar.activation(row[:, u * width : (u + 1) * width], acc[:], COPY, scale=scale)
                         else:
-                            nc.vector.tensor_scalar(row[:, HALF:], acc[:], scale, None, ALU.mult)
+                            nc.vector.tensor_scalar(row[:, u * width :], acc[:], scale, None, ALU.mult)
                 else:
-                    acc = bank(t + 1, [P, S])
+                    acc = bank(t + 3, [P, S])
                     product(acc[:], w_codes, w_scales, t, codes, scales, 0, S)
                     rows.append(acc)
             return rows
@@ -158,79 +163,133 @@ def tile_picked_lifted_none_po_kernel(
             for c in range(4):
                 quant(codes, scales, grouped, CH * c, CH * (c + 1))
 
-        r = layer("y", w1_c, w1_s, g_w, g_s, 0.5)
+        r = layer("y", w1_c, w1_s, g_w, g_s, 0.5, 4)
         rows = [r[0], r[1], r[3], r[5]]
         accs = [None, r[2], r[4], r[6]]
         z = [sb("z%d" % t, [P, S], F32) for t in range(PACK)]
         z_g = sb("z_g", [P, PACK * S], BF16)
         z_c = sb("z_c", [P, S], U32)
         z_s = sb("z_s", [P, S], U8)
-        nc.scalar.copy(
-            w3_dw[:].bitcast(U16).rearrange("p (t m) -> p m t", t=PACK), w3_w[:].bitcast(U16).rearrange("p (m t) -> p m t", t=PACK)
-        )
+        w3_w = sb("w1_g", [P, 2 * S], U8)
+        nc.sync.dma_start(w3_w[:].bitcast(I32), w3_words[0].bitcast(I32))
         ab = {}
 
+        def look(t):
+            ab[t] = fetch("y", t, rows[t], accs[t], 0.5, la_sb, lb_sb)
+
         def mean(t):
-            a, b = fetch("y", t, rows[t], accs[t], 0.5, la_sb, lb_sb)
-            ab[t] = (a, b)
+            a, b = ab[t]
             nc.vector.tensor_tensor(z[t][:].indirect(lb_sb[:]), a[:], b[:], ALU.add)
 
-        def diff(t):
+        terms = {}
+
+        def half_diff(t):
+            a, b = ab[t]
+            d = sb("y%d" % (t + 1), [P, V], F32)
+            nc.vector.tensor_tensor(d[:], b[:], a[:], ALU.subtract)
+            terms[t] = (d, d)
+
+        def doubled(t):
             a, b = ab[t]
             na = sb("na%d" % t, [P, V], F32)
             pb = sb("pb%d" % t, [P, V], F32)
             nc.scalar.activation(na[:], a[:], COPY, scale=-2.0)
             nc.scalar.activation(pb[:], b[:], COPY, scale=2.0)
-            nc.vector.tensor_tensor(z[t][:].indirect(la_sb[:]), pb[:], na[:], ALU.add)
+            terms[t] = (pb, na)
 
+        def put_diff(t):
+            nc.vector.tensor_tensor(z[t][:].indirect(la_sb[:]), terms[t][0][:], terms[t][1][:], ALU.add)
+
+        def diff(t):
+            doubled(t)
+            put_diff(t)
+
+        look(0)
         mean(0)
+        look(1)
+        half_diff(0)
         mean(1)
-        diff(0)
+        put_diff(0)
+        look(2)
+        half_diff(1)
         mean(2)
-        diff(1)
+        put_diff(1)
+        look(3)
         mean(3)
+        w2_g = sb("y3", [P, PACK * S], BF16)
         early_plane(z_g, z[0], 0)
         diff(2)
         deal(nc.scalar.copy, w2_g, w2_raw, 0, 0, 32)
+        deal(nc.scalar.copy, w2_g, w2_raw, 0, 32, 64)
         early_plane(z_g, z[1], 1)
         diff(3)
-        deal(nc.scalar.copy, w2_g, w2_raw, 0, 32, 64)
         deal(nc.scalar.copy, w2_g, w2_raw, 1, 0, 32)
-        deal(nc.vector.tensor_copy, w2_g, w2_raw, 1, 32, 64)
         early_plane(z_g, z[2], 2)
+        deal(nc.scalar.copy, w2_g, w2_raw, 1, 32, 64)
         quant(w2_c, w2_s, w2_g, 0, P)
         res_sb = load_halves(res)
         last_plane(z_g, z[3], z_c, z_s)
         for t in range(1, PACK):
             quant(w2_c, w2_s, w2_g, P * t, P * (t + 1))
-        w3_ds = sb("z_g", [P, S], U8)
-        nc.vector.tensor_copy(
-            w3_ds[:].rearrange("p (t m) -> p t m", t=PACK), w3_s[:].rearrange("p (m t) -> p t m", t=PACK)
-        )
 
-        r = layer("h", w2_c, w2_s, z_c, z_s, 1.0)
+        r = layer("h", w2_c, w2_s, z_c, z_s, 1.0, 4)
         rows = [r[0], r[1], r[3], r[5]]
         accs = [None, r[2], r[4], r[6]]
         z2 = [sb("zz%d" % t, [P, S], F32) for t in range(PACK)]
         z2_g = sb("z2_g", [P, PACK * S], BF16)
         z2_c = sb("z2_c", [P, S], U32)
         z2_s = sb("z2_s", [P, S], U8)
-        low = {}
-        for t in range(PACK + 1):
-            if t < PACK:
-                a, b = fetch("h", t, rows[t], accs[t], 1.0, ma_sb, mb_sb)
-                hi = sb("hi%d" % t, [P, V], F32)
-                lo = sb("lo%d" % t, [P, V], F32)
-                low[t] = lo
-                nc.vector.tensor_tensor(hi[:], a[:], b[:], ALU.max)
-                nc.vector.tensor_tensor(lo[:], a[:], b[:], ALU.min)
-                nc.vector.tensor_copy(z2[t][:].indirect(ma_sb[:]), hi[:])
-            if t > 0:
-                nc.vector.tensor_copy(z2[t - 1][:].indirect(mb_sb[:]), low[t - 1][:])
-            if t > 1:
-                early_plane(z2_g, z2[t - 2], t - 2)
-        last_plane(z2_g, z2[3], z2_c, z2_s)
+        ab2 = {}
+        gap = {}
+        rise = {}
 
+        def look2(t):
+            ab2[t] = fetch("h", t, rows[t], accs[t], 1.0, ma_sb, mb_sb)
+
+        def sub(t):
+            gap[t] = sb("gap%d" % t, [P, V], F32)
+            nc.vector.tensor_tensor(gap[t][:], ab2[t][1][:], ab2[t][0][:], ALU.subtract)
+
+        def put_hi(t):
+            rise[t] = sb("rise%d" % t, [P, V], F32)
+            nc.scalar.activation(rise[t][:], gap[t][:], RELU)
+            nc.vector.tensor_tensor(z2[t][:].indirect(ma_sb[:]), ab2[t][0][:], rise[t][:], ALU.add)
+
+        def put_lo(t):
+            fall = sb("fall%d" % t, [P, V], F32)
+            nc.scalar.activation(fall[:], rise[t][:], COPY, scale=-1.0)
+            nc.vector.tensor_tensor(z2[t][:].indirect(mb_sb[:]), ab2[t][1][:], fall[:], ALU.add)
+
+        look2(0)
+        hi0 = sb("hi0", [P, V], F32)
+        nc.vector.tensor_tensor(hi0[:], ab2[0][0][:], ab2[0][1][:], ALU.max)
+        nc.vector.tensor_copy(z2[0][:].indirect(ma_sb[:]), hi0[:])
+        look2(1)
+        lo0 = sb("h1", [P, V], F32)
+        nc.vector.tensor_tensor(lo0[:], ab2[0][0][:], ab2[0][1][:], ALU.min)
+        sub(1)
+        nc.vector.tensor_copy(z2[0][:].indirect(mb_sb[:]), lo0[:])
+        look2(2)
+        sub(2)
+        put_hi(1)
+        look2(3)
+        sub(3)
+        put_hi(2)
+        put_lo(1)
+        plane(nc.scalar.copy, z2_g, z2[0], 0, 0, S)
+        put_hi(3)
+        put_lo(2)
+        plane(nc.scalar.copy, z2_g, z2[1], 1, 0, S)
+        put_lo(3)
+        plane(nc.scalar.copy, z2_g, z2[2], 2, 0, S)
+        for c in range(4):
+            plane(nc.scalar.copy, z2_g, z2[3], 3, CH * c, CH * (c + 1))
+            quant(z2_c, z2_s, z2_g, CH * c, CH * (c + 1))
+
+        w3_dw = sb("y3", [P, 2 * S], U8)
+        nc.scalar.copy(
+            w3_dw[:].bitcast(U16).rearrange("p (t m) -> p m t", t=PACK), w3_w[:].bitcast(U16).rearrange("p (m t) -> p m t", t=PACK)
+        )
         o_g = sb("o_g", [P, PACK * S], BF16)
         o_c = sb("o_c", [P, S], U32)
         o_s = sb("o_s", [P, S], U8)
@@ -238,7 +297,7 @@ def tile_picked_lifted_none_po_kernel(
         out_words = out_1[0].rearrange("p n t -> p (n t)").bitcast(I32)
         for c in range(4):
             cols = slice(CH * c, CH * (c + 1))
-            acc = bank(c + 4 if c > 0 else 0, [P, PACK, CH])
+            acc = bank(c, [P, PACK, CH])
             for t in range(PACK):
                 nc.tensor.matmul_mx(
                     out=acc[:, t, :],
@@ -252,12 +311,13 @@ def tile_picked_lifted_none_po_kernel(
             o = sb("o%d" % c, [P, PACK, CH], F32)
             nc.vector.tensor_tensor(o[:], acc[:], res_sb[c // 2][:, :, CH * (c % 2) : CH * (c % 2 + 1)], ALU.add)
             nc.sync.dma_start(out_rows[:, :, cols], o[:])
-            nc.scalar.copy(
+            (nc.scalar.copy if c < 3 else nc.vector.tensor_copy)(
                 o_g[:, PACK * CH * c : PACK * CH * (c + 1)].rearrange("p (c i t) -> p c t i", i=4, t=PACK),
                 o[:].rearrange("p t (c i) -> p c t i", i=4),
             )
             quant(o_c, o_s, o_g, CH * c, CH * (c + 1))
-            nc.sync.dma_start(out_words[:, cols], o_c[:, cols].bitcast(I32))
+            if c % 2 == 1:
+                nc.sync.dma_start(out_words[:, CH * (c - 1) : CH * (c + 1)], o_c[:, CH * (c - 1) : CH * (c + 1)].bitcast(I32))
         for q in range(4):
-            eng = nc.sync if q % 2 == 0 else nc.scalar
+            eng = nc.sync if q % 2 == 1 else nc.scalar
             eng.dma_start(out_2[0, 4 * q : 4 * q + 4, :].bitcast(I32), o_s[32 * q : 32 * q + 4, :].bitcast(I32))

@@ -105,7 +105,8 @@ def tile_picked_lifted_none_po_kernel(
         w1_c = sb("w1_c", [P, S], U32)
         w1_s = sb("w1_s", [P, S], U8)
         deal(nc.scalar.copy, w1_g, w1_raw, 0, 0, 64)
-        deal(nc.vector.tensor_copy, w1_g, w1_raw, 1, 0, 64)
+        deal(nc.vector.tensor_copy, w1_g, w1_raw, 1, 0, 40)
+        deal(nc.scalar.copy, w1_g, w1_raw, 1, 40, 64)
         quant(w1_c, w1_s, w1_g, 0, S)
         for c in range(4):
             nc.vector.tensor_copy(g_w[:, CH * c : CH * (c + 1)], x_w[:].indirect(offs_sb[:, 8 * c : 8 * (c + 1)]))

@@ -16,12 +16,18 @@ RELU = mybir.ActivationFunctionType.Relu
 
 P = 128
 PACK = 4
+QUADS = 4
 T = 2048
 S = 512
 V = 256
-HALF = 256
-CH = 128
-FLOPS = 3 * 2 * 512 * 512 * 512
+HALF = S // 2
+CHUNK = 128
+CHUNKS = S // CHUNK
+STRIPE = 16
+M_HALF = HALF // PACK
+W1_ON_VECTOR = 40
+DIFF_ON_VECTOR = 2
+FLOPS = 3 * 2 * S * S * S
 
 
 def tile_picked_lifted_none_po_kernel(
@@ -33,114 +39,66 @@ def tile_picked_lifted_none_po_kernel(
         keep = ctx.enter_context(tc.tile_pool(name="keep", bufs=1))
         psum = ctx.enter_context(tc.psum_pool(name="psum", bufs=1))
 
-        def sb(name, shape, dtype):
-            return keep.tile(shape, dtype, name=name, align_bytes=64)
+        def sb(name, shape, dtype, tag=None):
+            return keep.tile(shape, dtype, name=name, tag=tag or name, align_bytes=64)
 
         def bank(n, shape):
             return psum.tile(shape, F32, name="bank%d" % n)
 
-        offs_sb = lists.tile([P, S // 16], U16, name="offs_sb")
-        la_sb = lists.tile([P, V // 16], U16, name="la_sb")
-        lb_sb = lists.tile([P, V // 16], U16, name="lb_sb")
-        ma_sb = lists.tile([P, V // 16], U16, name="ma_sb")
-        mb_sb = lists.tile([P, V // 16], U16, name="mb_sb")
-
-        x_w = sb("x_w", [P, T], U32)
-        x_s = sb("x_s", [P, T], U8)
-        w3_s = sb("w3_s", [P, S], U8)
-
-        def load_halves(src):
-            tiles = []
+        def load_halves(name, src):
+            halves = []
             for u in range(2):
-                raw = sb("raw%d" % u, [P, PACK, HALF], F32)
-                nc.sync.dma_start(raw[:], src.rearrange("(p j) c -> p j c", j=PACK)[:, :, u * HALF : (u + 1) * HALF])
-                tiles.append(raw)
-            return tiles
+                half = sb("%s_raw%d" % (name, u), [P, PACK, HALF], F32, tag="raw%d" % u)
+                nc.sync.dma_start(half[:], src.rearrange("(p j) c -> p j c", j=PACK)[:, :, u * HALF : (u + 1) * HALF])
+                halves.append(half)
+            return halves
 
-        nc.gpsimd.memset(x_s[:].bitcast(I32), 0)
-        nc.vector.memset(w3_s[:].bitcast(I32), 0)
-        nc.gpsimd.dma_start(w3_s[0:16, :].bitcast(I32), w3_scales[0].bitcast(I32))
-        w3_ds = sb("w3_ds", [P, S], U8)
-        nc.gpsimd.memset(w3_ds[:].bitcast(I32), 0)
-        for q in range(4):
-            nc.scalar.dma_start(x_s[32 * q : 32 * q + 4, :].bitcast(I32), x_scales[0, 4 * q : 4 * q + 4, :].bitcast(I32))
-        nc.sync.dma_start(offs_sb[:], offs)
-        nc.sync.dma_start(la_sb[:], la)
-        nc.sync.dma_start(lb_sb[:], lb)
-        nc.sync.dma_start(ma_sb[:], ma)
-        w1_raw = load_halves(w1)
-        nc.sync.dma_start(x_w[:].bitcast(I32), x_words[0].rearrange("p n t -> p (n t)").bitcast(I32))
-        nc.sync.dma_start(mb_sb[:], mb)
-        w3_rows = sb("w3_rows", [P, S], U8)
-        nc.vector.tensor_copy(
-            w3_rows[:].rearrange("p (t m) -> p t m", t=PACK), w3_s[:].rearrange("p (m t) -> p t m", t=PACK)
-        )
-        for q in range(4):
-            nc.sync.dma_start(w3_ds[32 * q : 32 * q + 4, :].bitcast(I32), w3_rows[4 * q : 4 * q + 4, :].bitcast(I32))
-
-        g_w = sb("g_w", [P, S], U32)
-        g_s = sb("g_s", [P, S], U8)
-        nc.vector.tensor_copy(g_s[:], x_s[:].indirect(offs_sb[:]))
-
-        def deal(copy, grouped, raw, u, m0, m1, t0=0, t1=PACK):
+        def deal(copy, grouped, halves, u, m0, m1):
             dst = grouped[:].rearrange("p (t m j) -> p m t j", t=PACK, j=PACK)
-            src = raw[u][:].rearrange("p j (m t) -> p m t j", t=PACK)
-            copy(dst[:, 64 * u + m0 : 64 * u + m1, t0:t1], src[:, m0:m1, t0:t1])
+            src = halves[u][:].rearrange("p j (m t) -> p m t j", t=PACK)
+            copy(dst[:, M_HALF * u + m0 : M_HALF * u + m1], src[:, m0:m1])
 
-        def quant(codes, scales, grouped, c0, c1):
-            nc.vector.quantize_mx(out=codes[:, c0:c1].bitcast(FP8X4), scales=scales[:, c0:c1], in_=grouped[:, PACK * c0 : PACK * c1])
+        def quantise(codes, scales, grouped, c0, c1):
+            nc.vector.quantize_mx(
+                out=codes[:, c0:c1].bitcast(FP8X4), scales=scales[:, c0:c1], in_=grouped[:, PACK * c0 : PACK * c1]
+            )
 
-        def product(out, w_codes, w_scales, t, codes, scales, c0, c1):
+        def product(out, w_codes, w_scales, t, codes, scales, cols):
             nc.tensor.matmul_mx(
                 out=out,
-                lhsT=w_codes[:, P * t : P * (t + 1)].bitcast(FP8X4),
+                lhsT=w_codes,
                 lhsT_scale=w_scales[:, P * t : P * (t + 1)],
-                rhs=codes[:, c0:c1].bitcast(FP8X4),
-                rhs_scale=scales[:, c0:c1],
+                rhs=codes[:, cols].bitcast(FP8X4),
+                rhs_scale=scales[:, cols],
                 start=True,
                 stop=True,
             )
 
-        w1_g = sb("w1_g", [P, PACK * S], BF16)
-        w1_c = sb("w1_c", [P, S], U32)
-        w1_s = sb("w1_s", [P, S], U8)
-        deal(nc.scalar.copy, w1_g, w1_raw, 0, 0, 64)
-        deal(nc.vector.tensor_copy, w1_g, w1_raw, 1, 0, 40)
-        deal(nc.scalar.copy, w1_g, w1_raw, 1, 40, 64)
-        quant(w1_c, w1_s, w1_g, 0, S)
-        for c in range(4):
-            nc.vector.tensor_copy(g_w[:, CH * c : CH * (c + 1)], x_w[:].indirect(offs_sb[:, 8 * c : 8 * (c + 1)]))
-
-        w2_raw = load_halves(w2)
-
-        w2_c = sb("w2_c", [P, S], U32)
-        w2_s = sb("w2_s", [P, S], U8)
-
-        def layer(name, w_codes, w_scales, codes, scales, scale, parts):
-            rows = []
+        def layer(name, w_codes, w_scales, codes, scales, factor):
+            tiles = []
             for t in range(PACK):
                 row = sb("%s%d" % (name, t), [P, S], F32)
-                rows.append(row)
                 if t == 0:
-                    width = S // parts
-                    for u in range(parts):
-                        acc = bank(u, [P, width])
-                        product(acc[:], w_codes, w_scales, t, codes, scales, u * width, (u + 1) * width)
-                        if u < parts - 1:
-                            nc.scalar.activation(row[:, u * width : (u + 1) * width], acc[:], COPY, scale=scale)
+                    for c in range(CHUNKS):
+                        cols = slice(CHUNK * c, CHUNK * (c + 1))
+                        acc = bank(c, [P, CHUNK])
+                        product(acc[:], w_codes[t].bitcast(FP8X4), w_scales, t, codes, scales, cols)
+                        if c < CHUNKS - 1:
+                            nc.scalar.activation(row[:, cols], acc[:], COPY, scale=factor)
                         else:
-                            nc.vector.tensor_scalar(row[:, u * width :], acc[:], scale, None, ALU.mult)
+                            nc.vector.tensor_scalar(row[:, cols], acc[:], factor, None, ALU.mult)
                 else:
-                    acc = bank(t + 3, [P, S])
-                    product(acc[:], w_codes, w_scales, t, codes, scales, 0, S)
-                    rows.append(acc)
-            return rows
+                    acc = bank(CHUNKS - 1 + t, [P, S])
+                    product(acc[:], w_codes[t].bitcast(FP8X4), w_scales, t, codes, scales, slice(0, S))
+                tiles.append((row, acc))
+            return tiles
 
-        def fetch(name, t, row, acc, scale, first, second):
+        def look_up(name, tiles, t, factor, first, second):
+            row, acc = tiles[t]
             a = sb("%s_a%d" % (name, t), [P, V], F32)
             b = sb("%s_b%d" % (name, t), [P, V], F32)
             if t > 0:
-                nc.scalar.activation(row[:], acc[:], COPY, scale=scale)
+                nc.scalar.activation(row[:], acc[:], COPY, scale=factor)
             nc.scalar.activation(a[:], row[:].indirect(first[:]), COPY)
             if t == 0:
                 nc.vector.tensor_copy(b[:], row[:].indirect(second[:]))
@@ -148,177 +106,193 @@ def tile_picked_lifted_none_po_kernel(
                 nc.scalar.activation(b[:], row[:].indirect(second[:]), COPY)
             return a, b
 
-        def plane(copy, grouped, z, t, c0, c1):
-            copy(grouped[:].rearrange("p (c j) -> p c j", j=PACK)[:, c0:c1, t], z[:, c0:c1])
+        def regroup(copy, grouped, tiles, t, c0, c1):
+            copy(grouped[:].rearrange("p (c j) -> p c j", j=PACK)[:, c0:c1, t], tiles[t][:, c0:c1])
 
-        def early_plane(grouped, z, t):
-            if t < 2:
-                plane(nc.scalar.copy, grouped, z, t, 0, S)
-            else:
-                plane(nc.vector.tensor_copy, grouped, z, t, 0, HALF)
-                plane(nc.scalar.copy, grouped, z, t, HALF, S)
+        offs_sb = lists.tile([P, S // STRIPE], U16, name="offs_sb")
+        la_sb = lists.tile([P, V // STRIPE], U16, name="la_sb")
+        lb_sb = lists.tile([P, V // STRIPE], U16, name="lb_sb")
+        ma_sb = lists.tile([P, V // STRIPE], U16, name="ma_sb")
+        mb_sb = lists.tile([P, V // STRIPE], U16, name="mb_sb")
 
-        def last_plane(grouped, z, codes, scales):
-            for c in range(4):
-                plane(nc.vector.tensor_copy if c < 2 else nc.scalar.copy, grouped, z, 3, CH * c, CH * (c + 1))
-            for c in range(4):
-                quant(codes, scales, grouped, CH * c, CH * (c + 1))
+        x_w = sb("x_w", [P, T], U32)
+        x_s = sb("x_s", [P, T], U8)
+        w3_s_raw = sb("w3_s_raw", [P, S], U8)
+        nc.gpsimd.memset(x_s[:].bitcast(I32), 0)
+        nc.vector.memset(w3_s_raw[:].bitcast(I32), 0)
+        nc.gpsimd.dma_start(w3_s_raw[0 : 4 * QUADS, :].bitcast(I32), w3_scales[0].bitcast(I32))
+        w3_s = sb("w3_s", [P, S], U8)
+        nc.gpsimd.memset(w3_s[:].bitcast(I32), 0)
+        for q in range(QUADS):
+            nc.scalar.dma_start(x_s[32 * q : 32 * q + 4, :].bitcast(I32), x_scales[0, 4 * q : 4 * q + 4, :].bitcast(I32))
+        nc.sync.dma_start(offs_sb[:], offs)
+        nc.sync.dma_start(la_sb[:], la)
+        nc.sync.dma_start(lb_sb[:], lb)
+        nc.sync.dma_start(ma_sb[:], ma)
+        w1_raw = load_halves("w1", w1)
+        nc.sync.dma_start(x_w[:].bitcast(I32), x_words[0].rearrange("p n t -> p (n t)").bitcast(I32))
+        nc.sync.dma_start(mb_sb[:], mb)
 
-        r = layer("y", w1_c, w1_s, g_w, g_s, 0.5, 4)
-        rows = [r[0], r[1], r[3], r[5]]
-        accs = [None, r[2], r[4], r[6]]
+        w3_s_dealt = sb("w3_s_dealt", [P, S], U8)
+        nc.vector.tensor_copy(
+            w3_s_dealt[:].rearrange("p (t m) -> p t m", t=PACK), w3_s_raw[:].rearrange("p (m t) -> p t m", t=PACK)
+        )
+        for q in range(QUADS):
+            nc.sync.dma_start(w3_s[32 * q : 32 * q + 4, :].bitcast(I32), w3_s_dealt[4 * q : 4 * q + 4, :].bitcast(I32))
+
+        picked_w = sb("picked_w", [P, S], U32)
+        picked_s = sb("picked_s", [P, S], U8)
+        nc.vector.tensor_copy(picked_s[:], x_s[:].indirect(offs_sb[:]))
+
+        w1_g = sb("w1_g", [P, PACK * S], BF16)
+        w1_c_first = sb("w1_c_first", [P, P], U32)
+        w1_s = sb("w1_s", [P, S], U8)
+        deal(nc.scalar.copy, w1_g, w1_raw, 0, 0, M_HALF)
+        deal(nc.vector.tensor_copy, w1_g, w1_raw, 1, 0, W1_ON_VECTOR)
+        deal(nc.scalar.copy, w1_g, w1_raw, 1, W1_ON_VECTOR, M_HALF)
+        quantise(w1_c_first, w1_s, w1_g, 0, P)
+        for c in range(CHUNKS):
+            entries = offs_sb[:, CHUNK // STRIPE * c : CHUNK // STRIPE * (c + 1)]
+            nc.vector.tensor_copy(picked_w[:, CHUNK * c : CHUNK * (c + 1)], x_w[:].indirect(entries))
+        w1_c_rest = sb("w1_c_rest", [P, S - P], U32, tag="x_w")
+        w1_c = [w1_c_first[:]] + [w1_c_rest[:, P * t : P * (t + 1)] for t in range(PACK - 1)]
+        for t in range(1, PACK):
+            nc.vector.quantize_mx(
+                out=w1_c[t].bitcast(FP8X4), scales=w1_s[:, P * t : P * (t + 1)], in_=w1_g[:, S * t : S * (t + 1)]
+            )
+
+        w2_raw = load_halves("w2", w2)
+        w2_c = sb("w2_c", [P, S], U32)
+        w2_s = sb("w2_s", [P, S], U8)
+
+        y = layer("y", w1_c, w1_s, picked_w, picked_s, 0.5)
         z = [sb("z%d" % t, [P, S], F32) for t in range(PACK)]
         z_g = sb("z_g", [P, PACK * S], BF16)
         z_c = sb("z_c", [P, S], U32)
         z_s = sb("z_s", [P, S], U8)
-        w3_w = sb("w1_g", [P, 2 * S], U8)
-        nc.sync.dma_start(w3_w[:].bitcast(I32), w3_words[0].bitcast(I32))
-        ab = {}
+        w3_w_raw = sb("w3_w_raw", [P, 2 * S], U8, tag="w1_g")
+        nc.sync.dma_start(w3_w_raw[:].bitcast(I32), w3_words[0].bitcast(I32))
 
-        def look(t):
-            ab[t] = fetch("y", t, rows[t], accs[t], 0.5, la_sb, lb_sb)
-
-        def mean(t):
-            a, b = ab[t]
+        y_pairs = []
+        for t in range(PACK):
+            a, b = look_up("y", y, t, 0.5, la_sb, lb_sb)
+            y_pairs.append((a, b))
+            previous_on_vector = 0 < t <= DIFF_ON_VECTOR
+            if previous_on_vector:
+                half_na = sb("half_na%d" % (t - 1), [P, V], F32, tag="y%d" % t)
+                nc.vector.tensor_tensor(half_na[:], y_pairs[t - 1][1][:], y_pairs[t - 1][0][:], ALU.subtract)
             nc.vector.tensor_tensor(z[t][:].indirect(lb_sb[:]), a[:], b[:], ALU.add)
+            if previous_on_vector:
+                nc.vector.tensor_tensor(z[t - 1][:].indirect(la_sb[:]), half_na[:], half_na[:], ALU.add)
 
-        terms = {}
+        def put_doubled_difference(t):
+            a, b = y_pairs[t]
+            minus_2a = sb("minus_2a%d" % t, [P, V], F32)
+            plus_2b = sb("plus_2b%d" % t, [P, V], F32)
+            nc.scalar.activation(minus_2a[:], a[:], COPY, scale=-2.0)
+            nc.scalar.activation(plus_2b[:], b[:], COPY, scale=2.0)
+            nc.vector.tensor_tensor(z[t][:].indirect(la_sb[:]), plus_2b[:], minus_2a[:], ALU.add)
 
-        def half_diff(t):
-            a, b = ab[t]
-            d = sb("y%d" % (t + 1), [P, V], F32)
-            nc.vector.tensor_tensor(d[:], b[:], a[:], ALU.subtract)
-            terms[t] = (d, d)
-
-        def doubled(t):
-            a, b = ab[t]
-            na = sb("na%d" % t, [P, V], F32)
-            pb = sb("pb%d" % t, [P, V], F32)
-            nc.scalar.activation(na[:], a[:], COPY, scale=-2.0)
-            nc.scalar.activation(pb[:], b[:], COPY, scale=2.0)
-            terms[t] = (pb, na)
-
-        def put_diff(t):
-            nc.vector.tensor_tensor(z[t][:].indirect(la_sb[:]), terms[t][0][:], terms[t][1][:], ALU.add)
-
-        def diff(t):
-            doubled(t)
-            put_diff(t)
-
-        look(0)
-        mean(0)
-        look(1)
-        half_diff(0)
-        mean(1)
-        put_diff(0)
-        look(2)
-        half_diff(1)
-        mean(2)
-        put_diff(1)
-        look(3)
-        mean(3)
-        w2_g = sb("y3", [P, PACK * S], BF16)
-        early_plane(z_g, z[0], 0)
-        diff(2)
-        deal(nc.scalar.copy, w2_g, w2_raw, 0, 0, 32)
-        deal(nc.scalar.copy, w2_g, w2_raw, 0, 32, 64)
-        early_plane(z_g, z[1], 1)
-        diff(3)
-        deal(nc.scalar.copy, w2_g, w2_raw, 1, 0, 32)
-        early_plane(z_g, z[2], 2)
-        deal(nc.scalar.copy, w2_g, w2_raw, 1, 32, 64)
-        quant(w2_c, w2_s, w2_g, 0, P)
-        res_sb = load_halves(res)
-        last_plane(z_g, z[3], z_c, z_s)
+        w2_g = sb("w2_g", [P, PACK * S], BF16, tag="y3")
+        piece = M_HALF // 2
+        regroup(nc.scalar.copy, z_g, z, 0, 0, S)
+        put_doubled_difference(2)
+        deal(nc.scalar.copy, w2_g, w2_raw, 0, 0, piece)
+        deal(nc.scalar.copy, w2_g, w2_raw, 0, piece, M_HALF)
+        regroup(nc.scalar.copy, z_g, z, 1, 0, S)
+        put_doubled_difference(3)
+        deal(nc.scalar.copy, w2_g, w2_raw, 1, 0, piece)
+        regroup(nc.vector.tensor_copy, z_g, z, 2, 0, HALF)
+        regroup(nc.scalar.copy, z_g, z, 2, HALF, S)
+        deal(nc.scalar.copy, w2_g, w2_raw, 1, piece, M_HALF)
+        quantise(w2_c, w2_s, w2_g, 0, P)
+        res_sb = load_halves("res", res)
+        for c in range(CHUNKS):
+            copy = nc.vector.tensor_copy if CHUNK * c < HALF else nc.scalar.copy
+            regroup(copy, z_g, z, 3, CHUNK * c, CHUNK * (c + 1))
+        for c in range(CHUNKS):
+            quantise(z_c, z_s, z_g, CHUNK * c, CHUNK * (c + 1))
         for t in range(1, PACK):
-            quant(w2_c, w2_s, w2_g, P * t, P * (t + 1))
+            quantise(w2_c, w2_s, w2_g, P * t, P * (t + 1))
 
-        r = layer("h", w2_c, w2_s, z_c, z_s, 1.0, 4)
-        rows = [r[0], r[1], r[3], r[5]]
-        accs = [None, r[2], r[4], r[6]]
-        z2 = [sb("zz%d" % t, [P, S], F32) for t in range(PACK)]
+        h = layer("h", [w2_c[:, P * t : P * (t + 1)] for t in range(PACK)], w2_s, z_c, z_s, 1.0)
+        z2 = [sb("z2_%d" % t, [P, S], F32) for t in range(PACK)]
         z2_g = sb("z2_g", [P, PACK * S], BF16)
         z2_c = sb("z2_c", [P, S], U32)
         z2_s = sb("z2_s", [P, S], U8)
-        ab2 = {}
-        gap = {}
+        h_pairs = {}
+        b_minus_a = {}
         rise = {}
 
-        def look2(t):
-            ab2[t] = fetch("h", t, rows[t], accs[t], 1.0, ma_sb, mb_sb)
+        def subtract(t):
+            a, b = h_pairs[t]
+            b_minus_a[t] = sb("b_minus_a%d" % t, [P, V], F32)
+            nc.vector.tensor_tensor(b_minus_a[t][:], b[:], a[:], ALU.subtract)
 
-        def sub(t):
-            gap[t] = sb("gap%d" % t, [P, V], F32)
-            nc.vector.tensor_tensor(gap[t][:], ab2[t][1][:], ab2[t][0][:], ALU.subtract)
-
-        def put_hi(t):
+        def put_larger(t):
             rise[t] = sb("rise%d" % t, [P, V], F32)
-            nc.scalar.activation(rise[t][:], gap[t][:], RELU)
-            nc.vector.tensor_tensor(z2[t][:].indirect(ma_sb[:]), ab2[t][0][:], rise[t][:], ALU.add)
+            nc.scalar.activation(rise[t][:], b_minus_a[t][:], RELU)
+            nc.vector.tensor_tensor(z2[t][:].indirect(ma_sb[:]), h_pairs[t][0][:], rise[t][:], ALU.add)
 
-        def put_lo(t):
+        def put_smaller(t):
             fall = sb("fall%d" % t, [P, V], F32)
             nc.scalar.activation(fall[:], rise[t][:], COPY, scale=-1.0)
-            nc.vector.tensor_tensor(z2[t][:].indirect(mb_sb[:]), ab2[t][1][:], fall[:], ALU.add)
+            nc.vector.tensor_tensor(z2[t][:].indirect(mb_sb[:]), h_pairs[t][1][:], fall[:], ALU.add)
 
-        look2(0)
-        hi0 = sb("hi0", [P, V], F32)
-        nc.vector.tensor_tensor(hi0[:], ab2[0][0][:], ab2[0][1][:], ALU.max)
-        nc.vector.tensor_copy(z2[0][:].indirect(ma_sb[:]), hi0[:])
-        look2(1)
-        lo0 = sb("h1", [P, V], F32)
-        nc.vector.tensor_tensor(lo0[:], ab2[0][0][:], ab2[0][1][:], ALU.min)
-        sub(1)
-        nc.vector.tensor_copy(z2[0][:].indirect(mb_sb[:]), lo0[:])
-        look2(2)
-        sub(2)
-        put_hi(1)
-        look2(3)
-        sub(3)
-        put_hi(2)
-        put_lo(1)
-        plane(nc.scalar.copy, z2_g, z2[0], 0, 0, S)
-        put_hi(3)
-        put_lo(2)
-        plane(nc.scalar.copy, z2_g, z2[1], 1, 0, S)
-        put_lo(3)
-        plane(nc.scalar.copy, z2_g, z2[2], 2, 0, S)
-        for c in range(4):
-            plane(nc.scalar.copy, z2_g, z2[3], 3, CH * c, CH * (c + 1))
-            quant(z2_c, z2_s, z2_g, CH * c, CH * (c + 1))
+        h_pairs[0] = look_up("h", h, 0, 1.0, ma_sb, mb_sb)
+        larger0 = sb("larger0", [P, V], F32)
+        nc.vector.tensor_tensor(larger0[:], h_pairs[0][0][:], h_pairs[0][1][:], ALU.max)
+        nc.vector.tensor_copy(z2[0][:].indirect(ma_sb[:]), larger0[:])
+        h_pairs[1] = look_up("h", h, 1, 1.0, ma_sb, mb_sb)
+        smaller0 = sb("smaller0", [P, V], F32, tag="h1")
+        nc.vector.tensor_tensor(smaller0[:], h_pairs[0][0][:], h_pairs[0][1][:], ALU.min)
+        subtract(1)
+        nc.vector.tensor_copy(z2[0][:].indirect(mb_sb[:]), smaller0[:])
+        for t in range(2, PACK):
+            h_pairs[t] = look_up("h", h, t, 1.0, ma_sb, mb_sb)
+            subtract(t)
+            put_larger(t - 1)
+        put_smaller(1)
+        regroup(nc.scalar.copy, z2_g, z2, 0, 0, S)
+        put_larger(3)
+        for t in range(2, PACK):
+            put_smaller(t)
+            regroup(nc.scalar.copy, z2_g, z2, t - 1, 0, S)
+        for c in range(CHUNKS):
+            regroup(nc.scalar.copy, z2_g, z2, 3, CHUNK * c, CHUNK * (c + 1))
+            quantise(z2_c, z2_s, z2_g, CHUNK * c, CHUNK * (c + 1))
 
-        w3_dw = sb("y3", [P, 2 * S], U8)
+        w3_w = sb("w3_w", [P, 2 * S], U8, tag="y3")
         nc.scalar.copy(
-            w3_dw[:].bitcast(U16).rearrange("p (t m) -> p m t", t=PACK), w3_w[:].bitcast(U16).rearrange("p (m t) -> p m t", t=PACK)
+            w3_w[:].bitcast(U16).rearrange("p (t m) -> p m t", t=PACK),
+            w3_w_raw[:].bitcast(U16).rearrange("p (m t) -> p m t", t=PACK),
         )
-        o_g = sb("o_g", [P, PACK * S], BF16)
-        o_c = sb("o_c", [P, S], U32)
-        o_s = sb("o_s", [P, S], U8)
+
+        out_g = sb("out_g", [P, PACK * S], BF16)
+        out_c = sb("out_c", [P, S], U32)
+        out_s = sb("out_s", [P, S], U8)
         out_rows = out_0.rearrange("(p t) j -> p t j", t=PACK)
         out_words = out_1[0].rearrange("p n t -> p (n t)").bitcast(I32)
-        for c in range(4):
-            cols = slice(CH * c, CH * (c + 1))
-            acc = bank(c, [P, PACK, CH])
+        per_half = HALF // CHUNK
+        for c in range(CHUNKS):
+            cols = slice(CHUNK * c, CHUNK * (c + 1))
+            u, within = divmod(c, per_half)
+            acc = bank(c, [P, PACK, CHUNK])
             for t in range(PACK):
-                nc.tensor.matmul_mx(
-                    out=acc[:, t, :],
-                    lhsT=w3_dw[:, 2 * P * t : 2 * P * (t + 1)].bitcast(FP4X4),
-                    lhsT_scale=w3_ds[:, P * t : P * (t + 1)],
-                    rhs=z2_c[:, cols].bitcast(FP8X4),
-                    rhs_scale=z2_s[:, cols],
-                    start=True,
-                    stop=True,
-                )
-            o = sb("o%d" % c, [P, PACK, CH], F32)
-            nc.vector.tensor_tensor(o[:], acc[:], res_sb[c // 2][:, :, CH * (c % 2) : CH * (c % 2 + 1)], ALU.add)
-            nc.sync.dma_start(out_rows[:, :, cols], o[:])
-            (nc.scalar.copy if c < 3 else nc.vector.tensor_copy)(
-                o_g[:, PACK * CH * c : PACK * CH * (c + 1)].rearrange("p (c i t) -> p c t i", i=4, t=PACK),
-                o[:].rearrange("p t (c i) -> p c t i", i=4),
+                w3_codes = w3_w[:, 2 * P * t : 2 * P * (t + 1)].bitcast(FP4X4)
+                product(acc[:, t, :], w3_codes, w3_s, t, z2_c, z2_s, cols)
+            total = sb("total%d" % c, [P, PACK, CHUNK], F32)
+            nc.vector.tensor_tensor(total[:], acc[:], res_sb[u][:, :, CHUNK * within : CHUNK * (within + 1)], ALU.add)
+            nc.sync.dma_start(out_rows[:, :, cols], total[:])
+            copy = nc.scalar.copy if c < CHUNKS - 1 else nc.vector.tensor_copy
+            copy(
+                out_g[:, PACK * CHUNK * c : PACK * CHUNK * (c + 1)].rearrange("p (g i t) -> p g t i", i=4, t=PACK),
+                total[:].rearrange("p t (g i) -> p g t i", i=4),
             )
-            quant(o_c, o_s, o_g, CH * c, CH * (c + 1))
-            if c % 2 == 1:
-                nc.sync.dma_start(out_words[:, CH * (c - 1) : CH * (c + 1)], o_c[:, CH * (c - 1) : CH * (c + 1)].bitcast(I32))
-        for q in range(4):
-            eng = nc.sync if q % 2 == 1 else nc.scalar
-            eng.dma_start(out_2[0, 4 * q : 4 * q + 4, :].bitcast(I32), o_s[32 * q : 32 * q + 4, :].bitcast(I32))
+            quantise(out_c, out_s, out_g, CHUNK * c, CHUNK * (c + 1))
+            if within == per_half - 1:
+                done = slice(HALF * u, HALF * (u + 1))
+                nc.sync.dma_start(out_words[:, done], out_c[:, done].bitcast(I32))
+        for q in range(QUADS):
+            queue = nc.scalar if q % 2 == 0 else nc.sync
+            queue.dma_start(out_2[0, 4 * q : 4 * q + 4, :].bitcast(I32), out_s[32 * q : 32 * q + 4, :].bitcast(I32))

from contextlib import ExitStack

import concourse.mybir as mybir

F32 = mybir.dt.float32
BF16 = mybir.dt.bfloat16
I32 = mybir.dt.int32
U32 = mybir.dt.uint32
U16 = mybir.dt.uint16
U8 = mybir.dt.uint8
FP8X4 = mybir.dt.float8_e4m3fn_x4
FP4X4 = mybir.dt.float4_e2m1fn_x4
ALU = mybir.AluOpType
COPY = mybir.ActivationFunctionType.Copy
RELU = mybir.ActivationFunctionType.Relu

P = 128
PACK = 4
QUADS = 4
T = 2048
S = 512
V = 256
HALF = S // 2
CHUNK = 128
CHUNKS = S // CHUNK
STRIPE = 16
M_HALF = HALF // PACK
W1_ON_VECTOR = 40
DIFF_ON_VECTOR = 2
FLOPS = 3 * 2 * S * S * S


def tile_picked_lifted_none_po_kernel(
    tc, x_words, x_scales, w1, w2, w3_words, w3_scales, res, offs, la, lb, ma, mb, out_0, out_1, out_2
):
    nc = tc.nc
    with ExitStack() as ctx:
        lists = ctx.enter_context(tc.tile_pool(name="lists", bufs=1))
        keep = ctx.enter_context(tc.tile_pool(name="keep", bufs=1))
        psum = ctx.enter_context(tc.psum_pool(name="psum", bufs=1))

        def sb(name, shape, dtype, tag=None):
            return keep.tile(shape, dtype, name=name, tag=tag or name, align_bytes=64)

        def bank(n, shape):
            return psum.tile(shape, F32, name="bank%d" % n)

        def load_halves(name, src):
            halves = []
            for u in range(2):
                half = sb("%s_raw%d" % (name, u), [P, PACK, HALF], F32, tag="raw%d" % u)
                nc.sync.dma_start(half[:], src.rearrange("(p j) c -> p j c", j=PACK)[:, :, u * HALF : (u + 1) * HALF])
                halves.append(half)
            return halves

        def deal(copy, grouped, halves, u, m0, m1):
            dst = grouped[:].rearrange("p (t m j) -> p m t j", t=PACK, j=PACK)
            src = halves[u][:].rearrange("p j (m t) -> p m t j", t=PACK)
            copy(dst[:, M_HALF * u + m0 : M_HALF * u + m1], src[:, m0:m1])

        def quantise(codes, scales, grouped, c0, c1):
            nc.vector.quantize_mx(
                out=codes[:, c0:c1].bitcast(FP8X4), scales=scales[:, c0:c1], in_=grouped[:, PACK * c0 : PACK * c1]
            )

        def product(out, w_codes, w_scales, t, codes, scales, cols):
            nc.tensor.matmul_mx(
                out=out,
                lhsT=w_codes,
                lhsT_scale=w_scales[:, P * t : P * (t + 1)],
                rhs=codes[:, cols].bitcast(FP8X4),
                rhs_scale=scales[:, cols],
                start=True,
                stop=True,
            )

        def layer(name, w_codes, w_scales, codes, scales, factor):
            tiles = []
            for t in range(PACK):
                row = sb("%s%d" % (name, t), [P, S], F32)
                if t == 0:
                    for c in range(CHUNKS):
                        cols = slice(CHUNK * c, CHUNK * (c + 1))
                        acc = bank(c, [P, CHUNK])
                        product(acc[:], w_codes[t].bitcast(FP8X4), w_scales, t, codes, scales, cols)
                        if c < CHUNKS - 1:
                            nc.scalar.activation(row[:, cols], acc[:], COPY, scale=factor)
                        else:
                            nc.vector.tensor_scalar(row[:, cols], acc[:], factor, None, ALU.mult)
                else:
                    acc = bank(CHUNKS - 1 + t, [P, S])
                    product(acc[:], w_codes[t].bitcast(FP8X4), w_scales, t, codes, scales, slice(0, S))
                tiles.append((row, acc))
            return tiles

        def look_up(name, tiles, t, factor, first, second):
            row, acc = tiles[t]
            a = sb("%s_a%d" % (name, t), [P, V], F32)
            b = sb("%s_b%d" % (name, t), [P, V], F32)
            if t > 0:
                nc.scalar.activation(row[:], acc[:], COPY, scale=factor)
            nc.scalar.activation(a[:], row[:].indirect(first[:]), COPY)
            if t == 0:
                nc.vector.tensor_copy(b[:], row[:].indirect(second[:]))
            else:
                nc.scalar.activation(b[:], row[:].indirect(second[:]), COPY)
            return a, b

        def regroup(copy, grouped, tiles, t, c0, c1):
            copy(grouped[:].rearrange("p (c j) -> p c j", j=PACK)[:, c0:c1, t], tiles[t][:, c0:c1])

        offs_sb = lists.tile([P, S // STRIPE], U16, name="offs_sb")
        la_sb = lists.tile([P, V // STRIPE], U16, name="la_sb")
        lb_sb = lists.tile([P, V // STRIPE], U16, name="lb_sb")
        ma_sb = lists.tile([P, V // STRIPE], U16, name="ma_sb")
        mb_sb = lists.tile([P, V // STRIPE], U16, name="mb_sb")

        x_w = sb("x_w", [P, T], U32)
        x_s = sb("x_s", [P, T], U8)
        w3_s_raw = sb("w3_s_raw", [P, S], U8)
        nc.gpsimd.memset(x_s[:].bitcast(I32), 0)
        nc.vector.memset(w3_s_raw[:].bitcast(I32), 0)
        nc.gpsimd.dma_start(w3_s_raw[0 : 4 * QUADS, :].bitcast(I32), w3_scales[0].bitcast(I32))
        w3_s = sb("w3_s", [P, S], U8)
        nc.gpsimd.memset(w3_s[:].bitcast(I32), 0)
        for q in range(QUADS):
            nc.scalar.dma_start(x_s[32 * q : 32 * q + 4, :].bitcast(I32), x_scales[0, 4 * q : 4 * q + 4, :].bitcast(I32))
        nc.sync.dma_start(offs_sb[:], offs)
        nc.sync.dma_start(la_sb[:], la)
        nc.sync.dma_start(lb_sb[:], lb)
        nc.sync.dma_start(ma_sb[:], ma)
        w1_raw = load_halves("w1", w1)
        nc.sync.dma_start(x_w[:].bitcast(I32), x_words[0].rearrange("p n t -> p (n t)").bitcast(I32))
        nc.sync.dma_start(mb_sb[:], mb)

        w3_s_dealt = sb("w3_s_dealt", [P, S], U8)
        nc.vector.tensor_copy(
            w3_s_dealt[:].rearrange("p (t m) -> p t m", t=PACK), w3_s_raw[:].rearrange("p (m t) -> p t m", t=PACK)
        )
        for q in range(QUADS):
            nc.sync.dma_start(w3_s[32 * q : 32 * q + 4, :].bitcast(I32), w3_s_dealt[4 * q : 4 * q + 4, :].bitcast(I32))

        picked_w = sb("picked_w", [P, S], U32)
        picked_s = sb("picked_s", [P, S], U8)
        nc.vector.tensor_copy(picked_s[:], x_s[:].indirect(offs_sb[:]))

        w1_g = sb("w1_g", [P, PACK * S], BF16)
        w1_c_first = sb("w1_c_first", [P, P], U32)
        w1_s = sb("w1_s", [P, S], U8)
        deal(nc.scalar.copy, w1_g, w1_raw, 0, 0, M_HALF)
        deal(nc.vector.tensor_copy, w1_g, w1_raw, 1, 0, W1_ON_VECTOR)
        deal(nc.scalar.copy, w1_g, w1_raw, 1, W1_ON_VECTOR, M_HALF)
        quantise(w1_c_first, w1_s, w1_g, 0, P)
        for c in range(CHUNKS):
            entries = offs_sb[:, CHUNK // STRIPE * c : CHUNK // STRIPE * (c + 1)]
            nc.vector.tensor_copy(picked_w[:, CHUNK * c : CHUNK * (c + 1)], x_w[:].indirect(entries))
        w1_c_rest = sb("w1_c_rest", [P, S - P], U32, tag="x_w")
        w1_c = [w1_c_first[:]] + [w1_c_rest[:, P * t : P * (t + 1)] for t in range(PACK - 1)]
        for t in range(1, PACK):
            nc.vector.quantize_mx(
                out=w1_c[t].bitcast(FP8X4), scales=w1_s[:, P * t : P * (t + 1)], in_=w1_g[:, S * t : S * (t + 1)]
            )

        w2_raw = load_halves("w2", w2)
        w2_c = sb("w2_c", [P, S], U32)
        w2_s = sb("w2_s", [P, S], U8)

        y = layer("y", w1_c, w1_s, picked_w, picked_s, 0.5)
        z = [sb("z%d" % t, [P, S], F32) for t in range(PACK)]
        z_g = sb("z_g", [P, PACK * S], BF16)
        z_c = sb("z_c", [P, S], U32)
        z_s = sb("z_s", [P, S], U8)
        w3_w_raw = sb("w3_w_raw", [P, 2 * S], U8, tag="w1_g")
        nc.sync.dma_start(w3_w_raw[:].bitcast(I32), w3_words[0].bitcast(I32))

        y_pairs = []
        for t in range(PACK):
            a, b = look_up("y", y, t, 0.5, la_sb, lb_sb)
            y_pairs.append((a, b))
            previous_on_vector = 0 < t <= DIFF_ON_VECTOR
            if previous_on_vector:
                half_na = sb("half_na%d" % (t - 1), [P, V], F32, tag="y%d" % t)
                nc.vector.tensor_tensor(half_na[:], y_pairs[t - 1][1][:], y_pairs[t - 1][0][:], ALU.subtract)
            nc.vector.tensor_tensor(z[t][:].indirect(lb_sb[:]), a[:], b[:], ALU.add)
            if previous_on_vector:
                nc.vector.tensor_tensor(z[t - 1][:].indirect(la_sb[:]), half_na[:], half_na[:], ALU.add)

        def put_doubled_difference(t):
            a, b = y_pairs[t]
            minus_2a = sb("minus_2a%d" % t, [P, V], F32)
            plus_2b = sb("plus_2b%d" % t, [P, V], F32)
            nc.scalar.activation(minus_2a[:], a[:], COPY, scale=-2.0)
            nc.scalar.activation(plus_2b[:], b[:], COPY, scale=2.0)
            nc.vector.tensor_tensor(z[t][:].indirect(la_sb[:]), plus_2b[:], minus_2a[:], ALU.add)

        w2_g = sb("w2_g", [P, PACK * S], BF16, tag="y3")
        piece = M_HALF // 2
        regroup(nc.scalar.copy, z_g, z, 0, 0, S)
        put_doubled_difference(2)
        deal(nc.scalar.copy, w2_g, w2_raw, 0, 0, piece)
        deal(nc.scalar.copy, w2_g, w2_raw, 0, piece, M_HALF)
        regroup(nc.scalar.copy, z_g, z, 1, 0, S)
        put_doubled_difference(3)
        deal(nc.scalar.copy, w2_g, w2_raw, 1, 0, piece)
        regroup(nc.vector.tensor_copy, z_g, z, 2, 0, HALF)
        regroup(nc.scalar.copy, z_g, z, 2, HALF, S)
        deal(nc.scalar.copy, w2_g, w2_raw, 1, piece, M_HALF)
        quantise(w2_c, w2_s, w2_g, 0, P)
        res_sb = load_halves("res", res)
        for c in range(CHUNKS):
            copy = nc.vector.tensor_copy if CHUNK * c < HALF else nc.scalar.copy
            regroup(copy, z_g, z, 3, CHUNK * c, CHUNK * (c + 1))
        for c in range(CHUNKS):
            quantise(z_c, z_s, z_g, CHUNK * c, CHUNK * (c + 1))
        for t in range(1, PACK):
            quantise(w2_c, w2_s, w2_g, P * t, P * (t + 1))

        h = layer("h", [w2_c[:, P * t : P * (t + 1)] for t in range(PACK)], w2_s, z_c, z_s, 1.0)
        z2 = [sb("z2_%d" % t, [P, S], F32) for t in range(PACK)]
        z2_g = sb("z2_g", [P, PACK * S], BF16)
        z2_c = sb("z2_c", [P, S], U32)
        z2_s = sb("z2_s", [P, S], U8)
        h_pairs = {}
        b_minus_a = {}
        rise = {}

        def subtract(t):
            a, b = h_pairs[t]
            b_minus_a[t] = sb("b_minus_a%d" % t, [P, V], F32)
            nc.vector.tensor_tensor(b_minus_a[t][:], b[:], a[:], ALU.subtract)

        def put_larger(t):
            rise[t] = sb("rise%d" % t, [P, V], F32)
            nc.scalar.activation(rise[t][:], b_minus_a[t][:], RELU)
            nc.vector.tensor_tensor(z2[t][:].indirect(ma_sb[:]), h_pairs[t][0][:], rise[t][:], ALU.add)

        def put_smaller(t):
            fall = sb("fall%d" % t, [P, V], F32)
            nc.scalar.activation(fall[:], rise[t][:], COPY, scale=-1.0)
            nc.vector.tensor_tensor(z2[t][:].indirect(mb_sb[:]), h_pairs[t][1][:], fall[:], ALU.add)

        h_pairs[0] = look_up("h", h, 0, 1.0, ma_sb, mb_sb)
        larger0 = sb("larger0", [P, V], F32)
        nc.vector.tensor_tensor(larger0[:], h_pairs[0][0][:], h_pairs[0][1][:], ALU.max)
        nc.vector.tensor_copy(z2[0][:].indirect(ma_sb[:]), larger0[:])
        h_pairs[1] = look_up("h", h, 1, 1.0, ma_sb, mb_sb)
        smaller0 = sb("smaller0", [P, V], F32, tag="h1")
        nc.vector.tensor_tensor(smaller0[:], h_pairs[0][0][:], h_pairs[0][1][:], ALU.min)
        subtract(1)
        nc.vector.tensor_copy(z2[0][:].indirect(mb_sb[:]), smaller0[:])
        for t in range(2, PACK):
            h_pairs[t] = look_up("h", h, t, 1.0, ma_sb, mb_sb)
            subtract(t)
            put_larger(t - 1)
        put_smaller(1)
        regroup(nc.scalar.copy, z2_g, z2, 0, 0, S)
        put_larger(3)
        for t in range(2, PACK):
            put_smaller(t)
            regroup(nc.scalar.copy, z2_g, z2, t - 1, 0, S)
        for c in range(CHUNKS):
            regroup(nc.scalar.copy, z2_g, z2, 3, CHUNK * c, CHUNK * (c + 1))
            quantise(z2_c, z2_s, z2_g, CHUNK * c, CHUNK * (c + 1))

        w3_w = sb("w3_w", [P, 2 * S], U8, tag="y3")
        nc.scalar.copy(
            w3_w[:].bitcast(U16).rearrange("p (t m) -> p m t", t=PACK),
            w3_w_raw[:].bitcast(U16).rearrange("p (m t) -> p m t", t=PACK),
        )

        out_g = sb("out_g", [P, PACK * S], BF16)
        out_c = sb("out_c", [P, S], U32)
        out_s = sb("out_s", [P, S], U8)
        out_rows = out_0.rearrange("(p t) j -> p t j", t=PACK)
        out_words = out_1[0].rearrange("p n t -> p (n t)").bitcast(I32)
        per_half = HALF // CHUNK
        for c in range(CHUNKS):
            cols = slice(CHUNK * c, CHUNK * (c + 1))
            u, within = divmod(c, per_half)
            acc = bank(c, [P, PACK, CHUNK])
            for t in range(PACK):
                w3_codes = w3_w[:, 2 * P * t : 2 * P * (t + 1)].bitcast(FP4X4)
                product(acc[:, t, :], w3_codes, w3_s, t, z2_c, z2_s, cols)
            total = sb("total%d" % c, [P, PACK, CHUNK], F32)
            nc.vector.tensor_tensor(total[:], acc[:], res_sb[u][:, :, CHUNK * within : CHUNK * (within + 1)], ALU.add)
            nc.sync.dma_start(out_rows[:, :, cols], total[:])
            copy = nc.scalar.copy if c < CHUNKS - 1 else nc.vector.tensor_copy
            copy(
                out_g[:, PACK * CHUNK * c : PACK * CHUNK * (c + 1)].rearrange("p (g i t) -> p g t i", i=4, t=PACK),
                total[:].rearrange("p t (g i) -> p g t i", i=4),
            )
            quantise(out_c, out_s, out_g, CHUNK * c, CHUNK * (c + 1))
            if within == per_half - 1:
                done = slice(HALF * u, HALF * (u + 1))
                nc.sync.dma_start(out_words[:, done], out_c[:, done].bitcast(I32))
        for q in range(QUADS):
            queue = nc.scalar if q % 2 == 0 else nc.sync
            queue.dma_start(out_2[0, 4 * q : 4 * q + 4, :].bitcast(I32), out_s[32 * q : 32 * q + 4, :].bitcast(I32))
